import numpy as np, ml_dtypes
CORES = [76,84,92,100,108,116,124]
N = 7
R, C = 2, 512
def setup_inputs(rng):
    return {"x": rng.standard_normal((N, 128, C), dtype=np.float32).astype(ml_dtypes.bfloat16), "u": rng.standard_normal((N, R, 128), dtype=np.float32).astype(ml_dtypes.bfloat16), "v": rng.standard_normal((N, R, C), dtype=np.float32).astype(ml_dtypes.bfloat16)}
def setup_inputs_big(rng):
    d = setup_inputs(rng)
    for k in ("u", "v"): d[k] = (d[k].astype(np.float32) * 1024.0).astype(d[k].dtype)
    for k in ("x",): d[k] = (d[k].astype(np.float32) * 1024.0 ** 2).astype(d[k].dtype)
    return d
def setup_inputs_small(rng):
    d = setup_inputs(rng)
    for k in ("u", "v"): d[k] = (d[k].astype(np.float32) * (1 / 1024.0)).astype(d[k].dtype)
    for k in ("x",): d[k] = (d[k].astype(np.float32) * (1 / 1024.0 ** 2)).astype(d[k].dtype)
    return d
def setup_inputs_apart(rng):
    d = setup_inputs(rng)
    f = (10.0 ** rng.permutation(np.linspace(-1.5, 1.5, N))).astype(np.float32).reshape(N, 1, 1)
    for k in ("u", "v"): d[k] = (d[k].astype(np.float32) * f).astype(d[k].dtype)
    for k in ("x",): d[k] = (d[k].astype(np.float32) * f * f).astype(d[k].dtype)
    return d
def reference(x, u, v):
    X, U, V = x.astype(np.float64), u.astype(np.float64), v.astype(np.float64)
    s = V.sum(axis=0)
    return {"y": np.stack([X[r] + U[r].T @ s for r in range(N)]).astype(ml_dtypes.bfloat16 if x.dtype != np.float64 else np.float64)}

from concourse.bass import DstId, RemoteDMATransfer
from concourse.mybir import AluOpType

N = 7
R, C = 2, 512
K = N * R
H = C // 2
RELAYS = 2

SCRATCH = {
    "land": ("dram", [N, 128, (R * C) // 128], "bfloat16"),
    "vs": ("sbuf", [128, C], "bfloat16"),
    "xs": ("sbuf", [128, C], "bfloat16"),
    "ys": ("sbuf", [128, C], "bfloat16"),
    "ub": ("sbuf", [128, R * 128], "bfloat16"),
    "sel": ("sbuf", [128, 16], "bfloat16"),
    "urep": ("sbuf", [128, 128], "bfloat16"),
    "psu": ("psum", [128, 512], "float32"),
    "ps0": ("psum", [128, 512], "float32"),
    "ps1": ("psum", [128, 512], "float32"),
}
SEMAPHORES = ["loaded", "uload", "xload", "selr", "umm", "urdy", "arrived", "sent",
              "gath", "mm0", "mm1", "vdone", "stored"]


def _plan(src, T, topo):
    others = [c for c in T.cores if c != src]
    direct = [c for c in others if topo.may_write(src, c)]
    cross = [c for c in others if not topo.may_write(src, c)]
    if not cross:
        return direct, []
    cand = [h for h in range(topo.CHIPS * topo.CORES_PER_CHIP)
            if topo.chip(h) == topo.chip(src) and T.rank_of(h) is None
            and all(topo.may_write(h, d) for d in cross)]
    cand.sort(key=lambda h: (topo.die(h) != topo.die(src), h))
    relays = cand[:RELAYS]
    k = (len(cross) + len(relays) - 1) // len(relays)
    shares = [(h, cross[i * k:(i + 1) * k]) for i, h in enumerate(relays)]
    return direct, [(h, d) for h, d in shares if d]


def _engine(src, dsts, topo):
    m = topo.mask(src, dsts[0])
    for d in dsts[1:]:
        m &= topo.mask(src, d)
    return m & -m


def _send(g, dsts, slot, engine, T, topo):
    ids = []
    for d in dsts:
        rid, pid, _ = topo.addr(d)
        ids.append(DstId(rid=rid, pnc=pid))
    g.remote_dma_fused(
        [RemoteDMATransfer(dst_ids=ids, dma_engine_mask=engine, remote_sem=T.sem.arrived,
                           srcs=[T.land[slot]], dsts=[T.land[slot] for _ in dsts], alu_op=0)],
        local_sem=T.sem.sent)


def rank_program(g, core, T, topo):
    S = T.sem
    rank = T.rank_of(core)

    if rank is None:
        for src in T.cores:
            if topo.chip(src) != topo.chip(core):
                continue
            for h, dsts in _plan(src, T, topo)[1]:
                if h == core:
                    g.wait_ge(S.arrived, 1)
                    _send(g, dsts, T.rank_of(src), _engine(core, dsts, topo), T, topo)
                    g.wait_ge(S.sent, 1)
        return

    sy, sc, te, ve = g.sync, g.scalar, g.tensor, g.vector
    direct, shares = _plan(core, T, topo)
    relays = [h for h, _ in shares]

    sy.dma_start(T.land[rank], T.v[:]).then_inc(S.loaded, 16)
    sc.dma_start(T.ub[0:1, :], T.u[:]).then_inc(S.uload, 16)
    sc.dma_start(T.xs[:], T.x[:]).then_inc(S.xload, 16)

    engine = _engine(core, relays + direct, topo)
    calls = 0
    g.wait_ge(S.loaded, 16)
    for dsts in (relays, direct):
        if dsts:
            _send(g, dsts, rank, engine, T, topo)
            calls += 1

    ve.memset(T.sel[0:1, 0:16:2], 1.0).then_inc(S.selr, 1)
    ve.memset(T.sel[0:1, 1:16:2], 0.0).then_inc(S.selr, 1)
    te.wait_ge(S.selr, 2)
    te.wait_ge(S.uload, 16)
    te.matmul(T.psu[0:K, 0:128], T.sel[0:1, 0:K], T.ub[0:1, 0:128], True, False)
    te.matmul(T.psu[0:K, 0:128], T.sel[0:1, 1:K + 1], T.ub[0:1, 128:256], False, True).then_inc(S.umm, 1)
    ve.wait_ge(S.umm, 1)
    ve.tensor_copy(T.urep[0:K, :], T.psu[0:K, 0:128]).then_inc(S.urdy, 1)
    te.wait_ge(S.urdy, 1)

    sy.wait_ge(S.loaded, 16)
    sy.wait_ge(S.arrived, N - 1)
    sy.dma_start(T.vs[0:K, :], T.land[:]).then_inc(S.gath, 16)

    te.wait_ge(S.gath, 16)
    te.matmul(T.ps0[:, 0:H], T.urep[0:K, :], T.vs[0:K, 0:H], True, True).then_inc(S.mm0, 1)
    te.matmul(T.ps1[:, 0:H], T.urep[0:K, :], T.vs[0:K, H:C], True, True).then_inc(S.mm1, 1)
    ve.wait_ge(S.xload, 16)
    ve.wait_ge(S.mm0, 1)
    ve.tensor_tensor(T.ys[:, 0:H], T.ps0[:, 0:H], T.xs[:, 0:H], AluOpType.add).then_inc(S.vdone, 1)
    ve.wait_ge(S.mm1, 1)
    ve.tensor_tensor(T.ys[:, H:C], T.ps1[:, 0:H], T.xs[:, H:C], AluOpType.add).then_inc(S.vdone, 1)

    sy.wait_ge(S.vdone, 2)
    sy.dma_start(T.y[:], T.ys[:]).then_inc(S.stored, 16)
    sy.wait_ge(S.stored, 16)
    g.wait_ge(S.sent, calls)
